import numpy as np
import ml_dtypes


def mxq(x, axis, fmt="e4m3"):
    dtype, down = {"e4m3": (ml_dtypes.float8_e4m3fn, 7), "e5m2": (ml_dtypes.float8_e5m2, 14)}[fmt]
    v = np.moveaxis(np.asarray(x, np.float32).astype(ml_dtypes.bfloat16).astype(np.float64), axis, -1)
    blocks = v.reshape(v.shape[:-1] + (-1, 32))
    amax = np.abs(blocks).max(-1, keepdims=True)
    byte = np.maximum(np.where(amax > 0, np.frexp(amax)[1] - 1 + 127, 0) - down, 1)
    scale = np.exp2(byte - 127.0)
    codes = (blocks / scale).astype(np.float32).astype(dtype).astype(np.float64)
    return np.moveaxis((codes * scale).reshape(v.shape), -1, axis)


WIDE = False


def mx_kscale(k):
    if not WIDE:
        return np.ones(k)
    levels = np.array([10, -10, 5, -5, 0])
    if k % 512:
        return np.exp2(np.random.permutation(np.resize(levels, k // 32))).repeat(32)
    a = np.empty((k // 512, 16))
    for p in range(k // 512):
        a[p, :8] = np.random.permutation(np.resize(levels, 8))
        for g in range(8):
            far = levels[np.abs(levels - a[p, g]) >= 10]
            a[p, g + 8] = far[np.random.randint(len(far))]
    return np.exp2(a.ravel()).repeat(32)


def f64(x):
    return np.asarray(x).astype(np.float64)


def striped(idx):
    return np.tile(idx.reshape(-1, 16).T, (8, 1)).astype(np.uint16)


def unstriped(offs):
    return offs[:16].T.reshape(-1).astype(np.int64)


def striped8(idx):
    return np.concatenate([x.reshape(-1, 16).T for x in idx]).astype(np.uint16)


def runs(offs, k):
    lists = np.stack([offs[16 * r : 16 * r + 16].T.reshape(-1) for r in range(8)]).astype(np.int64)
    return lists[np.arange(k) % 512 // 64]


def pack_weight(w):
    k, n = w.shape
    w = f64(np.asarray(w, np.float32).astype(ml_dtypes.bfloat16)).reshape(k // 32, 32, n)
    amax = np.abs(w).max(1)
    byte = np.clip(np.where(amax > 0, np.frexp(amax)[1] - 1 + 127 - 7, 1), 1, 254)
    scaled = (w * np.exp2(127.0 - byte)[:, None, :]).reshape(k, n).astype(np.float32)
    words = np.ascontiguousarray(scaled.reshape(k // 512, 128, 4, n).transpose(0, 1, 3, 2)).astype(ml_dtypes.float8_e4m3fn).view(np.uint8)
    return words, np.ascontiguousarray(byte.astype(np.uint8).reshape(k // 512, 16, n))


def unpack_weight(words, scales):
    g, p, n, _ = words.shape
    vals = np.ascontiguousarray(words).view(ml_dtypes.float8_e4m3fn).astype(np.float64) * np.repeat(np.exp2(scales.astype(np.float64) - 127.0), 8, axis=1)[..., None]
    return vals.transpose(0, 1, 3, 2).reshape(g * 512, n)


K, T, S, N, G, H, U = 512, 1024, 512, 512, 2048, 512, 1024


def setup_inputs():
    n = np.random.standard_normal
    s = mx_kscale(K)[:, None]
    u = mx_kscale(S)
    packed_xT = pack_weight(n((K, T)) * s)
    packed_dT = pack_weight(n((K, G)) / s)
    return {
        "x_words": packed_xT[0],
        "x_scales": packed_xT[1],
        "d_words": packed_dT[0],
        "d_scales": packed_dT[1],
        "gn": (np.random.uniform(0.5, 1.5, (H, 1)) * u[:, None]).astype(np.float32),
        "w1": (n((H, N)) / np.sqrt(H) / u[:, None]).astype(np.float32),
        "mem": n((N, U)).astype(np.float32),
        "offs": striped(np.random.permutation(T)[:S]),
        "k1": striped8(np.random.randint(0, G, (8, H))),
        "two": striped(np.random.permutation(T)[:S]),
        "k2": striped8(np.random.randint(0, G, (8, H))),
        "n1": striped8(np.stack([np.random.permutation(S) for _ in range(8)])),
        "n2": striped8(np.stack([np.random.permutation(S) for _ in range(8)])),
        "n3": striped8(np.stack([np.random.permutation(S) for _ in range(8)])),
        "n4": striped8(np.stack([np.random.permutation(S) for _ in range(8)])),
        "n5": striped(np.random.permutation(U)[:S]),
    }


def reference(x_words, x_scales, d_words, d_scales, gn, w1, mem, offs, k1, two, k2, n1, n2, n3, n4, n5):
    d_k1 = unpack_weight(d_words, d_scales)[np.arange(K)[:, None], runs(k1, K)]
    xq = unpack_weight(x_words, x_scales)[:, unstriped(offs)]
    a = 0.0625 * (d_k1.T @ xq)
    d_k2 = unpack_weight(d_words, d_scales)[np.arange(K)[:, None], runs(k2, K)]
    x_two = unpack_weight(x_words, x_scales)[:, unstriped(two)]
    b = 0.0625 * (d_k2.T @ x_two)
    z = f64(gn) * (np.maximum(a[np.arange(H)[:, None], runs(n1, H)] + b[np.arange(H)[:, None], runs(n3, H)], a[np.arange(H)[:, None], runs(n2, H)] + b[np.arange(H)[:, None], runs(n4, H)]))
    h = mxq(f64(w1), 0, "e4m3").T @ mxq(z, 0, "e4m3")
    nw = np.maximum(h, 0.5 * f64(mem)[:, unstriped(n5)])
    out = f64(mem).copy()
    out[:, unstriped(n5)] = nw
    return out

@@ -1,0 +1,150 @@
+from contextlib import ExitStack
+
+import concourse.mybir as mybir
+
+K, T, S, N, G, H, U = 512, 1024, 512, 512, 2048, 512, 1024
+FLOPS = 3 * 2 * 512 * 512 * 512
+
+F32 = mybir.dt.float32
+BF16 = mybir.dt.bfloat16
+I32 = mybir.dt.int32
+U32 = mybir.dt.uint32
+U16 = mybir.dt.uint16
+U8 = mybir.dt.uint8
+FP8X4 = mybir.dt.float8_e4m3fn_x4
+COPY = mybir.ActivationFunctionType.Copy
+ALU = mybir.AluOpType
+
+P = 128
+PACK = 4
+HALVES = 2
+W = S // HALVES
+LIST_COLS = S // 16
+
+
+def tile_picked_twpqpathbpagex_none_p_kernel(tc, x_words, x_scales, d_words, d_scales, gn, w1, mem, offs, k1, two, k2, n1, n2, n3, n4, n5, out):
+    nc = tc.nc
+    with ExitStack() as ctx:
+        keep = ctx.enter_context(tc.tile_pool(name="keep", bufs=1))
+        psum = ctx.enter_context(tc.psum_pool(name="psum", bufs=8))
+
+        def load_list(name, src):
+            lst = keep.tile([P, LIST_COLS], U16, name=name)
+            nc.sync.dma_start(lst[:], src)
+            return lst
+
+        d_bytes = keep.tile([P, G], U8, name="d_bytes", align_bytes=64)
+        x_bytes = keep.tile([P, T], U8, name="x_bytes", align_bytes=64)
+
+        k1_l = load_list("k1_l", k1)
+        d_rows = d_scales[0].bitcast(I32).rearrange("(r s) c -> s r c", s=2)
+        for s in range(2):
+            nc.sync.dma_start(d_bytes[s:P:2, :].bitcast(I32), d_rows[s].unsqueeze(1).broadcast_to([8, 8, G // 4]))
+        x_tab = keep.tile([P, T], U32, name="x_tab", align_bytes=64)
+        nc.sync.dma_start(x_tab[:].bitcast(I32), x_words[0].rearrange("p n t -> p (n t)").bitcast(I32))
+        offs_l = load_list("offs_l", offs)
+        d_tab = keep.tile([P, G], U32, name="d_tab", align_bytes=64)
+        nc.sync.dma_start(d_tab[:].bitcast(I32), d_words[0].rearrange("p n t -> p (n t)").bitcast(I32))
+        x_rows = x_scales[0].bitcast(I32).rearrange("(q s) c -> s q c", s=4)
+        for s in range(4):
+            nc.scalar.dma_start(x_bytes[s:P:4, :].bitcast(I32), x_rows[s].unsqueeze(1).broadcast_to([4, 8, T // 4]))
+        n5_l = load_list("n5_l", n5)
+        pages = []
+        for t in range(PACK):
+            page = keep.tile([P, U], F32, name="page%d" % t)
+            nc.sync.dma_start(page[:], mem[P * t : P * (t + 1), :])
+            pages.append(page)
+        n1_l = load_list("n1_l", n1)
+        n2_l = load_list("n2_l", n2)
+        k2_l = load_list("k2_l", k2)
+        two_l = load_list("two_l", two)
+        n3_l = load_list("n3_l", n3)
+        n4_l = load_list("n4_l", n4)
+        gain = keep.tile([P, PACK], F32, name="gain")
+        nc.sync.dma_start(gain[:], gn.rearrange("(p t) o -> p (t o)", t=PACK))
+        w_raw = keep.tile([P, PACK, N], F32, name="w_raw")
+        nc.sync.dma_start(w_raw[:], w1.rearrange("(p j) m -> p j m", j=PACK))
+
+        def coded_product(name, d_list, x_list, queue):
+            ds_g = keep.tile([P, H], U8, name=name + "_ds_g", align_bytes=64)
+            nc.vector.tensor_copy(ds_g[:], d_bytes[:].indirect(d_list[:]))
+            ds = keep.tile([P, H], U8, name=name + "_ds", align_bytes=64)
+            nc.vector.tensor_copy(ds[:].rearrange("p (t m) -> p m t", t=PACK), ds_g[:].rearrange("p (m t) -> p m t", t=PACK))
+            for s in range(2):
+                queue.dma_start(ds[2 + s : P : 32, :].bitcast(I32), ds[16 + s : P : 32, :].bitcast(I32))
+            xw = keep.tile([P, S], U32, name=name + "_xw", align_bytes=64)
+            nc.vector.tensor_copy(xw[:], x_tab[:].indirect(x_list[:]))
+            xs = keep.tile([P, S], U8, name=name + "_xs", align_bytes=64)
+            nc.vector.tensor_copy(xs[:], x_bytes[:].indirect(x_list[:]))
+            dw_g = keep.tile([P, H], U32, name=name + "_dw_g", align_bytes=64)
+            nc.vector.tensor_copy(dw_g[:], d_tab[:].indirect(d_list[:]))
+            dw = keep.tile([P, H], U32, name=name + "_dw", align_bytes=64)
+            nc.vector.tensor_copy(dw[:].rearrange("p (t m) -> p m t", t=PACK), dw_g[:].rearrange("p (m t) -> p m t", t=PACK))
+            rows = []
+            for t in range(PACK):
+                cols = slice(P * t, P * (t + 1))
+                acc = psum.tile([P, S], F32, name="acc")
+                nc.tensor.matmul_mx(out=acc[:], lhsT=dw[:, cols].bitcast(FP8X4), lhsT_scale=ds[:, cols], rhs=xw[:].bitcast(FP8X4), rhs_scale=xs[:], start=True, stop=True)
+                row = keep.tile([P, S], F32, name="%s_row%d" % (name, t))
+                nc.vector.tensor_scalar(row[:], acc[:], 0.0625, None, ALU.mult)
+                rows.append(row)
+            return rows
+
+        old = []
+        for t in range(PACK):
+            o = keep.tile([P, S], F32, name="old%d" % t)
+            nc.scalar.activation(o[:], pages[t][:].indirect(n5_l[:]), COPY)
+            old.append(o)
+
+        def fetch(name, rows, lists, hf):
+            got = []
+            for t in range(PACK):
+                g = keep.tile([P, 2, W], F32, name="%s_got%d_%d" % (name, hf, t))
+                for u in range(2):
+                    nc.scalar.activation(g[:, u, :], rows[t][:].indirect(lists[u][:, 16 * hf : 16 * (hf + 1)]), COPY)
+                got.append(g)
+            return got
+
+        a_rows = coded_product("a", k1_l, offs_l, nc.gpsimd)
+        a_got = [fetch("a", a_rows, (n1_l, n2_l), hf) for hf in range(HALVES)]
+        b_rows = coded_product("b", k2_l, two_l, nc.gpsimd)
+
+        w_bf = keep.tile([P, N, PACK], BF16, name="w_bf", align_bytes=64)
+        nc.vector.tensor_copy(w_bf[:].rearrange("p (c i) j -> p c j i", i=4), w_raw[:].rearrange("p j (c i) -> p c j i", i=4))
+        w_codes = keep.tile([P, N], U32, name="w_codes", align_bytes=64)
+        w_scale = keep.tile([P, N], U8, name="w_scale", align_bytes=64)
+        nc.vector.quantize_mx(out=w_codes[:].bitcast(FP8X4), scales=w_scale[:], in_=w_bf[:].rearrange("p m j -> p (m j)"))
+
+        news = []
+        for hf in range(HALVES):
+            b_got = fetch("b", b_rows, (n3_l, n4_l), hf)
+            big = keep.tile([P, PACK, W], F32, name="big%d" % hf)
+            for t in range(PACK):
+                sums = keep.tile([P, 2, W], F32, name="sums%d_%d" % (hf, t))
+                nc.vector.tensor_tensor(sums[:], a_got[hf][t][:], b_got[t][:], ALU.add)
+                nc.vector.tensor_tensor(big[:, t, :], sums[:, 0, :], sums[:, 1, :], ALU.max)
+            z_bf = keep.tile([P, W, PACK], BF16, name="z_bf%d" % hf, align_bytes=64)
+            nc.vector.tensor_tensor(
+                z_bf[:].rearrange("p (c i) t -> p c t i", i=4),
+                big[:].rearrange("p t (c i) -> p c t i", i=4),
+                gain[:].unsqueeze(1).unsqueeze(3).broadcast_to([P, W // 4, PACK, 4]),
+                ALU.mult,
+            )
+            z_codes = keep.tile([P, W], U32, name="z_codes%d" % hf, align_bytes=64)
+            z_scale = keep.tile([P, W], U8, name="z_scale%d" % hf, align_bytes=64)
+            nc.vector.quantize_mx(out=z_codes[:].bitcast(FP8X4), scales=z_scale[:], in_=z_bf[:].rearrange("p c t -> p (c t)"))
+            new = []
+            for t in range(PACK):
+                cols = slice(P * t, P * (t + 1))
+                acc = psum.tile([P, W], F32, name="acc")
+                nc.tensor.matmul_mx(out=acc[:], lhsT=w_codes[:, cols].bitcast(FP8X4), lhsT_scale=w_scale[:, cols], rhs=z_codes[:].bitcast(FP8X4), rhs_scale=z_scale[:], start=True, stop=True)
+                nw = keep.tile([P, W], F32, name="nw%d_%d" % (hf, t))
+                nc.vector.scalar_tensor_tensor(nw[:], old[t][:, W * hf : W * (hf + 1)], 0.5, acc[:], ALU.mult, ALU.max)
+                new.append(nw)
+            news.append(new)
+
+        for hf in range(HALVES):
+            for t in range(PACK):
+                nc.scalar.activation(pages[t][:].indirect(n5_l[:, 16 * hf : 16 * (hf + 1)]), news[hf][t][:], COPY)
+                if hf == HALVES - 1:
+                    nc.sync.dma_start(out[P * t : P * (t + 1), :], pages[t][:])

@@ -36,65 +36,70 @@ def tile_picked_twpqpathbpagex_none_p_kernel(tc, x_words, x_scales, d_words, d_s
         d_bytes = keep.tile([P, G], U8, name="d_bytes", align_bytes=64)
         x_bytes = keep.tile([P, T], U8, name="x_bytes", align_bytes=64)
 
+        gn_raw = keep.tile([P, PACK], F32, name="gn_raw")
+        nc.gpsimd.dma_start(gn_raw[:], gn.rearrange("(p t) o -> p (t o)", t=PACK))
+        gain = keep.tile([P, PACK], F32, name="gain")
+        nc.scalar.activation(gain[:], gn_raw[:], COPY, scale=0.0625)
+        def load_scale_rows(table, src, width):
+            rows = src[0].bitcast(I32).rearrange("(r s) c -> s r c", s=2)
+            for s in range(2):
+                nc.sync.dma_start(table[s:P:2, :].bitcast(I32), rows[s].unsqueeze(1).broadcast_to([8, 8, width // 4]))
+
+        pages = [keep.tile([P, U], F32, name="page%d" % t) for t in range(PACK)]
+
+        def load_page(t):
+            nc.sync.dma_start(pages[t][:], mem[P * t : P * (t + 1), :])
+
         k1_l = load_list("k1_l", k1)
-        d_rows = d_scales[0].bitcast(I32).rearrange("(r s) c -> s r c", s=2)
-        for s in range(2):
-            nc.sync.dma_start(d_bytes[s:P:2, :].bitcast(I32), d_rows[s].unsqueeze(1).broadcast_to([8, 8, G // 4]))
-        x_tab = keep.tile([P, T], U32, name="x_tab", align_bytes=64)
-        nc.sync.dma_start(x_tab[:].bitcast(I32), x_words[0].rearrange("p n t -> p (n t)").bitcast(I32))
+        load_scale_rows(d_bytes, d_scales, G)
         offs_l = load_list("offs_l", offs)
+        load_scale_rows(x_bytes, x_scales, T)
+        x_tab = keep.tile([P, T], U32, name="x_tab", tag="x_tab", align_bytes=64)
+        nc.sync.dma_start(x_tab[:].bitcast(I32), x_words[0].rearrange("p n t -> p (n t)").bitcast(I32))
+        load_page(0)
         d_tab = keep.tile([P, G], U32, name="d_tab", align_bytes=64)
         nc.sync.dma_start(d_tab[:].bitcast(I32), d_words[0].rearrange("p n t -> p (n t)").bitcast(I32))
-        x_rows = x_scales[0].bitcast(I32).rearrange("(q s) c -> s q c", s=4)
-        for s in range(4):
-            nc.scalar.dma_start(x_bytes[s:P:4, :].bitcast(I32), x_rows[s].unsqueeze(1).broadcast_to([4, 8, T // 4]))
         n5_l = load_list("n5_l", n5)
-        pages = []
-        for t in range(PACK):
-            page = keep.tile([P, U], F32, name="page%d" % t)
-            nc.sync.dma_start(page[:], mem[P * t : P * (t + 1), :])
-            pages.append(page)
+        load_page(1)
+        load_page(2)
         n1_l = load_list("n1_l", n1)
         n2_l = load_list("n2_l", n2)
+        load_page(3)
         k2_l = load_list("k2_l", k2)
         two_l = load_list("two_l", two)
         n3_l = load_list("n3_l", n3)
         n4_l = load_list("n4_l", n4)
-        gain = keep.tile([P, PACK], F32, name="gain")
-        nc.sync.dma_start(gain[:], gn.rearrange("(p t) o -> p (t o)", t=PACK))
-        w_raw = keep.tile([P, PACK, N], F32, name="w_raw")
-        nc.sync.dma_start(w_raw[:], w1.rearrange("(p j) m -> p j m", j=PACK))
 
-        def coded_product(name, d_list, x_list, queue):
-            ds_g = keep.tile([P, H], U8, name=name + "_ds_g", align_bytes=64)
+        def coded_product(name, d_list, x_list, queue, rows, tags):
+            ds_g = keep.tile([P, H], U8, name=name + "_ds_g", tag=tags[4], align_bytes=64)
             nc.vector.tensor_copy(ds_g[:], d_bytes[:].indirect(d_list[:]))
-            ds = keep.tile([P, H], U8, name=name + "_ds", align_bytes=64)
-            nc.vector.tensor_copy(ds[:].rearrange("p (t m) -> p m t", t=PACK), ds_g[:].rearrange("p (m t) -> p m t", t=PACK))
+            xs_g = keep.tile([P, S], U8, name=name + "_xs_g", tag=tags[2], align_bytes=64)
+            nc.vector.tensor_copy(xs_g[:], x_bytes[:].indirect(x_list[:]))
+            plane = keep.tile([P, H + S], U8, name=name + "_plane", tag=tags[3], align_bytes=64)
+            ds = plane[:, 0:H]
+            xs = plane[:, H : H + S]
+            nc.vector.tensor_copy(ds.rearrange("p (t m) -> p m t", t=PACK), ds_g[:].rearrange("p (m t) -> p m t", t=PACK))
+            nc.vector.tensor_copy(xs.bitcast(I32), xs_g[:].bitcast(I32))
             for s in range(2):
-                queue.dma_start(ds[2 + s : P : 32, :].bitcast(I32), ds[16 + s : P : 32, :].bitcast(I32))
-            xw = keep.tile([P, S], U32, name=name + "_xw", align_bytes=64)
+                queue.dma_start(plane[2 + s : P : 32, :].bitcast(I32), plane[16 + s : P : 32, :].bitcast(I32))
+            xw = keep.tile([P, S], U32, name=name + "_xw", tag=tags[5], align_bytes=64)
             nc.vector.tensor_copy(xw[:], x_tab[:].indirect(x_list[:]))
-            xs = keep.tile([P, S], U8, name=name + "_xs", align_bytes=64)
-            nc.vector.tensor_copy(xs[:], x_bytes[:].indirect(x_list[:]))
-            dw_g = keep.tile([P, H], U32, name=name + "_dw_g", align_bytes=64)
+            dw_g = keep.tile([P, H], U32, name=name + "_dw_g", tag=tags[0], align_bytes=64)
             nc.vector.tensor_copy(dw_g[:], d_tab[:].indirect(d_list[:]))
-            dw = keep.tile([P, H], U32, name=name + "_dw", align_bytes=64)
+            dw = keep.tile([P, H], U32, name=name + "_dw", tag=tags[1], align_bytes=64)
             nc.vector.tensor_copy(dw[:].rearrange("p (t m) -> p m t", t=PACK), dw_g[:].rearrange("p (m t) -> p m t", t=PACK))
-            rows = []
             for t in range(PACK):
                 cols = slice(P * t, P * (t + 1))
                 acc = psum.tile([P, S], F32, name="acc")
-                nc.tensor.matmul_mx(out=acc[:], lhsT=dw[:, cols].bitcast(FP8X4), lhsT_scale=ds[:, cols], rhs=xw[:].bitcast(FP8X4), rhs_scale=xs[:], start=True, stop=True)
-                row = keep.tile([P, S], F32, name="%s_row%d" % (name, t))
-                nc.vector.tensor_scalar(row[:], acc[:], 0.0625, None, ALU.mult)
-                rows.append(row)
-            return rows
+                nc.tensor.matmul_mx(out=acc[:], lhsT=dw[:, cols].bitcast(FP8X4), lhsT_scale=ds[:, cols], rhs=xw[:].bitcast(FP8X4), rhs_scale=xs, start=True, stop=True)
+                nc.vector.tensor_copy(rows[t][:, 0:S], acc[:])
 
-        old = []
+        a_rows = [keep.tile([P, 2 * S], F32, name="a_rows%d" % t) for t in range(PACK)]
+        b_rows = [keep.tile([P, S], F32, name="b_rows%d" % t) for t in range(PACK)]
+        old = [[a_rows[2 * (t % 2) + hf][:, S + W * (t // 2) : S + W * (t // 2 + 1)] for hf in range(HALVES)] for t in range(PACK)]
         for t in range(PACK):
-            o = keep.tile([P, S], F32, name="old%d" % t)
-            nc.scalar.activation(o[:], pages[t][:].indirect(n5_l[:]), COPY)
-            old.append(o)
+            for hf in range(HALVES):
+                nc.scalar.activation(old[t][hf], pages[t][:].indirect(n5_l[:, 16 * hf : 16 * (hf + 1)]), COPY)
 
         def fetch(name, rows, lists, hf):
             got = []
@@ -105,11 +110,18 @@ def tile_picked_twpqpathbpagex_none_p_kernel(tc, x_words, x_scales, d_words, d_s
                 got.append(g)
             return got
 
-        a_rows = coded_product("a", k1_l, offs_l, nc.gpsimd)
-        a_got = [fetch("a", a_rows, (n1_l, n2_l), hf) for hf in range(HALVES)]
-        b_rows = coded_product("b", k2_l, two_l, nc.gpsimd)
+        coded_product("a", k1_l, offs_l, nc.scalar, a_rows, ("dw0", "dw1", "sc0", "sc1", "sc3", "xw"))
+        a_got = []
+        for t in range(PACK):
+            g = keep.tile([P, 2, S], F32, name="a_got%d" % t)
+            for u, lst in enumerate((n1_l, n2_l)):
+                nc.scalar.activation(g[:, u, :], a_rows[t][:].indirect(lst[:]), COPY)
+            a_got.append(g)
+        coded_product("b", k2_l, two_l, nc.sync, b_rows, ("dw1", "dw0", "sc1", "sc2", "xw", "xw"))
 
-        w_bf = keep.tile([P, N, PACK], BF16, name="w_bf", align_bytes=64)
+        w_raw = keep.tile([P, PACK, N], F32, name="w_raw", tag="x_tab", align_bytes=64)
+        nc.sync.dma_start(w_raw[:], w1.rearrange("(p j) m -> p j m", j=PACK))
+        w_bf = keep.tile([P, N, PACK], BF16, name="w_bf", tag="dw0", align_bytes=64)
         nc.vector.tensor_copy(w_bf[:].rearrange("p (c i) j -> p c j i", i=4), w_raw[:].rearrange("p j (c i) -> p c j i", i=4))
         w_codes = keep.tile([P, N], U32, name="w_codes", align_bytes=64)
         w_scale = keep.tile([P, N], U8, name="w_scale", align_bytes=64)
@@ -121,7 +133,7 @@ def tile_picked_twpqpathbpagex_none_p_kernel(tc, x_words, x_scales, d_words, d_s
             big = keep.tile([P, PACK, W], F32, name="big%d" % hf)
             for t in range(PACK):
                 sums = keep.tile([P, 2, W], F32, name="sums%d_%d" % (hf, t))
-                nc.vector.tensor_tensor(sums[:], a_got[hf][t][:], b_got[t][:], ALU.add)
+                nc.vector.tensor_tensor(sums[:], a_got[t][:, :, W * hf : W * (hf + 1)], b_got[t][:], ALU.add)
                 nc.vector.tensor_tensor(big[:, t, :], sums[:, 0, :], sums[:, 1, :], ALU.max)
             z_bf = keep.tile([P, W, PACK], BF16, name="z_bf%d" % hf, align_bytes=64)
             nc.vector.tensor_tensor(
@@ -139,7 +151,7 @@ def tile_picked_twpqpathbpagex_none_p_kernel(tc, x_words, x_scales, d_words, d_s
                 acc = psum.tile([P, W], F32, name="acc")
                 nc.tensor.matmul_mx(out=acc[:], lhsT=w_codes[:, cols].bitcast(FP8X4), lhsT_scale=w_scale[:, cols], rhs=z_codes[:].bitcast(FP8X4), rhs_scale=z_scale[:], start=True, stop=True)
                 nw = keep.tile([P, W], F32, name="nw%d_%d" % (hf, t))
-                nc.vector.scalar_tensor_tensor(nw[:], old[t][:, W * hf : W * (hf + 1)], 0.5, acc[:], ALU.mult, ALU.max)
+                nc.vector.scalar_tensor_tensor(nw[:], old[t][hf], 0.5, acc[:], ALU.mult, ALU.max)
                 new.append(nw)
             news.append(new)
 

@@ -36,30 +36,33 @@ def tile_picked_twpqpathbpagex_none_p_kernel(tc, x_words, x_scales, d_words, d_s
         d_bytes = keep.tile([P, G], U8, name="d_bytes", align_bytes=64)
         x_bytes = keep.tile([P, T], U8, name="x_bytes", align_bytes=64)
 
+        nc.gpsimd.memset(d_bytes[:].bitcast(I32), 0)
+        nc.vector.memset(x_bytes[:].bitcast(I32), 0)
         gn_raw = keep.tile([P, PACK], F32, name="gn_raw")
         nc.gpsimd.dma_start(gn_raw[:], gn.rearrange("(p t) o -> p (t o)", t=PACK))
-        gain = keep.tile([P, PACK], F32, name="gain")
-        nc.scalar.activation(gain[:], gn_raw[:], COPY, scale=0.0625)
-        def load_scale_rows(table, src, width):
+
+        def load_scale_rows(table, src):
             rows = src[0].bitcast(I32).rearrange("(r s) c -> s r c", s=2)
             for s in range(2):
-                nc.sync.dma_start(table[s:P:2, :].bitcast(I32), rows[s].unsqueeze(1).broadcast_to([8, 8, width // 4]))
+                nc.scalar.dma_start(table[s:P:16, :].bitcast(I32), rows[s])
 
         pages = [keep.tile([P, U], F32, name="page%d" % t) for t in range(PACK)]
 
         def load_page(t):
             nc.sync.dma_start(pages[t][:], mem[P * t : P * (t + 1), :])
 
+        load_scale_rows(d_bytes, d_scales)
+        load_scale_rows(x_bytes, x_scales)
+        gain = keep.tile([P, PACK], F32, name="gain")
+        nc.scalar.activation(gain[:], gn_raw[:], COPY, scale=0.0625)
         k1_l = load_list("k1_l", k1)
-        load_scale_rows(d_bytes, d_scales, G)
         offs_l = load_list("offs_l", offs)
-        load_scale_rows(x_bytes, x_scales, T)
         x_tab = keep.tile([P, T], U32, name="x_tab", tag="x_tab", align_bytes=64)
         nc.sync.dma_start(x_tab[:].bitcast(I32), x_words[0].rearrange("p n t -> p (n t)").bitcast(I32))
+        n5_l = load_list("n5_l", n5)
         load_page(0)
         d_tab = keep.tile([P, G], U32, name="d_tab", align_bytes=64)
         nc.sync.dma_start(d_tab[:].bitcast(I32), d_words[0].rearrange("p n t -> p (n t)").bitcast(I32))
-        n5_l = load_list("n5_l", n5)
         load_page(1)
         load_page(2)
         n1_l = load_list("n1_l", n1)
@@ -130,18 +133,15 @@ def tile_picked_twpqpathbpagex_none_p_kernel(tc, x_words, x_scales, d_words, d_s
         news = []
         for hf in range(HALVES):
             b_got = fetch("b", b_rows, (n3_l, n4_l), hf)
-            big = keep.tile([P, PACK, W], F32, name="big%d" % hf)
+            z_rows = keep.tile([P, PACK, W], BF16, name="z_rows%d" % hf)
             for t in range(PACK):
                 sums = keep.tile([P, 2, W], F32, name="sums%d_%d" % (hf, t))
                 nc.vector.tensor_tensor(sums[:], a_got[t][:, :, W * hf : W * (hf + 1)], b_got[t][:], ALU.add)
-                nc.vector.tensor_tensor(big[:, t, :], sums[:, 0, :], sums[:, 1, :], ALU.max)
+                big = keep.tile([P, W], F32, name="big%d_%d" % (hf, t))
+                nc.vector.tensor_tensor(big[:], sums[:, 0, :], sums[:, 1, :], ALU.max)
+                nc.vector.tensor_scalar(z_rows[:, t, :], big[:], gain[:, t : t + 1], None, ALU.mult)
             z_bf = keep.tile([P, W, PACK], BF16, name="z_bf%d" % hf, align_bytes=64)
-            nc.vector.tensor_tensor(
-                z_bf[:].rearrange("p (c i) t -> p c t i", i=4),
-                big[:].rearrange("p t (c i) -> p c t i", i=4),
-                gain[:].unsqueeze(1).unsqueeze(3).broadcast_to([P, W // 4, PACK, 4]),
-                ALU.mult,
-            )
+            nc.vector.tensor_copy(z_bf[:].rearrange("p (c i) t -> p c t i", i=4), z_rows[:].rearrange("p t (c i) -> p c t i", i=4))
             z_codes = keep.tile([P, W], U32, name="z_codes%d" % hf, align_bytes=64)
             z_scale = keep.tile([P, W], U8, name="z_scale%d" % hf, align_bytes=64)
             nc.vector.quantize_mx(out=z_codes[:].bitcast(FP8X4), scales=z_scale[:], in_=z_bf[:].rearrange("p c t -> p (c t)"))

@@ -41,68 +41,71 @@ def tile_picked_twpqpathbpagex_none_p_kernel(tc, x_words, x_scales, d_words, d_s
         gn_raw = keep.tile([P, PACK], F32, name="gn_raw")
         nc.gpsimd.dma_start(gn_raw[:], gn.rearrange("(p t) o -> p (t o)", t=PACK))
 
-        def load_scale_rows(table, src):
-            rows = src[0].bitcast(I32).rearrange("(r s) c -> s r c", s=2)
-            for s in range(2):
-                nc.scalar.dma_start(table[s:P:16, :].bitcast(I32), rows[s])
-
         pages = [keep.tile([P, U], F32, name="page%d" % t) for t in range(PACK)]
 
         def load_page(t):
             nc.sync.dma_start(pages[t][:], mem[P * t : P * (t + 1), :])
 
-        load_scale_rows(d_bytes, d_scales)
-        load_scale_rows(x_bytes, x_scales)
+        d_rows = d_scales[0].bitcast(I32).rearrange("(r s) c -> s r c", s=2)
+        for s in range(2):
+            nc.scalar.dma_start(d_bytes[s:P:16, :].bitcast(I32), d_rows[s])
+        x_rows = x_scales[0].bitcast(I32)
+        for q in range(4):
+            nc.scalar.dma_start(x_bytes[32 * q : 32 * q + 4, :].bitcast(I32), x_rows[4 * q : 4 * q + 4, :])
         gain = keep.tile([P, PACK], F32, name="gain")
         nc.scalar.activation(gain[:], gn_raw[:], COPY, scale=0.0625)
         k1_l = load_list("k1_l", k1)
         offs_l = load_list("offs_l", offs)
         x_tab = keep.tile([P, T], U32, name="x_tab", tag="x_tab", align_bytes=64)
         nc.sync.dma_start(x_tab[:].bitcast(I32), x_words[0].rearrange("p n t -> p (n t)").bitcast(I32))
-        n5_l = load_list("n5_l", n5)
         load_page(0)
         d_tab = keep.tile([P, G], U32, name="d_tab", align_bytes=64)
         nc.sync.dma_start(d_tab[:].bitcast(I32), d_words[0].rearrange("p n t -> p (n t)").bitcast(I32))
-        load_page(1)
-        load_page(2)
+        n5_l = load_list("n5_l", n5)
+        k2_l = load_list("k2_l", k2)
+        for t in range(1, PACK):
+            load_page(t)
         n1_l = load_list("n1_l", n1)
         n2_l = load_list("n2_l", n2)
-        load_page(3)
-        k2_l = load_list("k2_l", k2)
         two_l = load_list("two_l", two)
         n3_l = load_list("n3_l", n3)
         n4_l = load_list("n4_l", n4)
 
         def coded_product(name, d_list, x_list, queue, rows, tags):
-            ds_g = keep.tile([P, H], U8, name=name + "_ds_g", tag=tags[4], align_bytes=64)
+            ds_g = keep.tile([P, H], U8, name=name + "_ds_g", align_bytes=64)
             nc.vector.tensor_copy(ds_g[:], d_bytes[:].indirect(d_list[:]))
-            xs_g = keep.tile([P, S], U8, name=name + "_xs_g", tag=tags[2], align_bytes=64)
-            nc.vector.tensor_copy(xs_g[:], x_bytes[:].indirect(x_list[:]))
-            plane = keep.tile([P, H + S], U8, name=name + "_plane", tag=tags[3], align_bytes=64)
-            ds = plane[:, 0:H]
-            xs = plane[:, H : H + S]
-            nc.vector.tensor_copy(ds.rearrange("p (t m) -> p m t", t=PACK), ds_g[:].rearrange("p (m t) -> p m t", t=PACK))
-            nc.vector.tensor_copy(xs.bitcast(I32), xs_g[:].bitcast(I32))
+            ds = keep.tile([P, H], U8, name=name + "_ds", align_bytes=64)
+            nc.vector.tensor_copy(ds[:].rearrange("p (t m) -> p m t", t=PACK), ds_g[:].rearrange("p (m t) -> p m t", t=PACK))
             for s in range(2):
-                queue.dma_start(plane[2 + s : P : 32, :].bitcast(I32), plane[16 + s : P : 32, :].bitcast(I32))
-            xw = keep.tile([P, S], U32, name=name + "_xw", tag=tags[5], align_bytes=64)
+                queue.dma_start(ds[2 + s : P : 32, :].bitcast(I32), ds[16 + s : P : 32, :].bitcast(I32))
+            xw = keep.tile([P, S], U32, name=name + "_xw", tag="xw", align_bytes=64)
             nc.vector.tensor_copy(xw[:], x_tab[:].indirect(x_list[:]))
             dw_g = keep.tile([P, H], U32, name=name + "_dw_g", tag=tags[0], align_bytes=64)
             nc.vector.tensor_copy(dw_g[:], d_tab[:].indirect(d_list[:]))
             dw = keep.tile([P, H], U32, name=name + "_dw", tag=tags[1], align_bytes=64)
             nc.vector.tensor_copy(dw[:].rearrange("p (t m) -> p m t", t=PACK), dw_g[:].rearrange("p (m t) -> p m t", t=PACK))
+            xs = keep.tile([P, S], U8, name=name + "_xs", tag="xs", align_bytes=64)
+            nc.vector.tensor_copy(xs[:], x_bytes[:].indirect(x_list[:]))
             for t in range(PACK):
                 cols = slice(P * t, P * (t + 1))
                 acc = psum.tile([P, S], F32, name="acc")
-                nc.tensor.matmul_mx(out=acc[:], lhsT=dw[:, cols].bitcast(FP8X4), lhsT_scale=ds[:, cols], rhs=xw[:].bitcast(FP8X4), rhs_scale=xs, start=True, stop=True)
+                nc.tensor.matmul_mx(out=acc[:], lhsT=dw[:, cols].bitcast(FP8X4), lhsT_scale=ds[:, cols], rhs=xw[:].bitcast(FP8X4), rhs_scale=xs[:], start=True, stop=True)
                 nc.vector.tensor_copy(rows[t][:, 0:S], acc[:])
 
-        a_rows = [keep.tile([P, 2 * S], F32, name="a_rows%d" % t) for t in range(PACK)]
+        last = PACK - 1
+        Q = S // PACK
+        a_rows = [keep.tile([P, 2 * S + Q], F32, name="a_rows%d" % t) for t in range(PACK)]
+        nc.gpsimd.memset(a_rows[last][:, S : 2 * S], 0.0)
         b_rows = [keep.tile([P, S], F32, name="b_rows%d" % t) for t in range(PACK)]
-        old = [[a_rows[2 * (t % 2) + hf][:, S + W * (t // 2) : S + W * (t // 2 + 1)] for hf in range(HALVES)] for t in range(PACK)]
-        for t in range(PACK):
-            for hf in range(HALVES):
-                nc.scalar.activation(old[t][hf], pages[t][:].indirect(n5_l[:, 16 * hf : 16 * (hf + 1)]), COPY)
+        for t in range(last):
+            nc.scalar.activation(a_rows[t][:, S : 2 * S], pages[t][:].indirect(n5_l[:]), COPY)
+        for q in range(PACK):
+            nc.scalar.activation(a_rows[q][:, 2 * S :], pages[last][:].indirect(n5_l[:, 8 * q : 8 * (q + 1)]), COPY)
+
+        def old_pieces(t, hf):
+            if t < last:
+                return [(slice(0, W), a_rows[t][:, S + W * hf : S + W * (hf + 1)])]
+            return [(slice(Q * u, Q * (u + 1)), a_rows[2 * hf + u][:, 2 * S :]) for u in range(2)]
 
         def fetch(name, rows, lists, hf):
             got = []
@@ -113,14 +116,14 @@ def tile_picked_twpqpathbpagex_none_p_kernel(tc, x_words, x_scales, d_words, d_s
                 got.append(g)
             return got
 
-        coded_product("a", k1_l, offs_l, nc.scalar, a_rows, ("dw0", "dw1", "sc0", "sc1", "sc3", "xw"))
+        coded_product("a", k1_l, offs_l, nc.scalar, a_rows, ("dw0", "dw1"))
         a_got = []
         for t in range(PACK):
             g = keep.tile([P, 2, S], F32, name="a_got%d" % t)
             for u, lst in enumerate((n1_l, n2_l)):
                 nc.scalar.activation(g[:, u, :], a_rows[t][:].indirect(lst[:]), COPY)
             a_got.append(g)
-        coded_product("b", k2_l, two_l, nc.sync, b_rows, ("dw1", "dw0", "sc1", "sc2", "xw", "xw"))
+        coded_product("b", k2_l, two_l, nc.sync, b_rows, ("dw1", "dw0"))
 
         w_raw = keep.tile([P, PACK, N], F32, name="w_raw", tag="x_tab", align_bytes=64)
         nc.sync.dma_start(w_raw[:], w1.rearrange("(p j) m -> p j m", j=PACK))
@@ -133,15 +136,20 @@ def tile_picked_twpqpathbpagex_none_p_kernel(tc, x_words, x_scales, d_words, d_s
         news = []
         for hf in range(HALVES):
             b_got = fetch("b", b_rows, (n3_l, n4_l), hf)
-            z_rows = keep.tile([P, PACK, W], BF16, name="z_rows%d" % hf)
-            for t in range(PACK):
-                sums = keep.tile([P, 2, W], F32, name="sums%d_%d" % (hf, t))
-                nc.vector.tensor_tensor(sums[:], a_got[t][:, :, W * hf : W * (hf + 1)], b_got[t][:], ALU.add)
-                big = keep.tile([P, W], F32, name="big%d_%d" % (hf, t))
-                nc.vector.tensor_tensor(big[:], sums[:, 0, :], sums[:, 1, :], ALU.max)
-                nc.vector.tensor_scalar(z_rows[:, t, :], big[:], gain[:, t : t + 1], None, ALU.mult)
-            z_bf = keep.tile([P, W, PACK], BF16, name="z_bf%d" % hf, align_bytes=64)
-            nc.vector.tensor_copy(z_bf[:].rearrange("p (c i) t -> p c t i", i=4), z_rows[:].rearrange("p t (c i) -> p c t i", i=4))
+            sums = keep.tile([P, PACK, 2, W], F32, name="sums%d" % hf, tag="stage%d" % hf, align_bytes=64)
+            big = keep.tile([P, PACK, W], F32, name="big%d" % hf)
+            for t in range(PACK + 1):
+                if t < PACK:
+                    nc.vector.tensor_tensor(sums[:, t], a_got[t][:, :, W * hf : W * (hf + 1)], b_got[t][:], ALU.add)
+                if t > 0:
+                    nc.vector.tensor_tensor(big[:, t - 1, :], sums[:, t - 1, 0, :], sums[:, t - 1, 1, :], ALU.max)
+            z_bf = keep.tile([P, W, PACK], BF16, name="z_bf%d" % hf, tag="stage%d" % (hf + 1), align_bytes=64)
+            nc.vector.tensor_tensor(
+                z_bf[:].rearrange("p (c i) t -> p c t i", i=4),
+                big[:].rearrange("p t (c i) -> p c t i", i=4),
+                gain[:].unsqueeze(1).unsqueeze(3).broadcast_to([P, W // 4, PACK, 4]),
+                ALU.mult,
+            )
             z_codes = keep.tile([P, W], U32, name="z_codes%d" % hf, align_bytes=64)
             z_scale = keep.tile([P, W], U8, name="z_scale%d" % hf, align_bytes=64)
             nc.vector.quantize_mx(out=z_codes[:].bitcast(FP8X4), scales=z_scale[:], in_=z_bf[:].rearrange("p c t -> p (c t)"))
@@ -151,7 +159,8 @@ def tile_picked_twpqpathbpagex_none_p_kernel(tc, x_words, x_scales, d_words, d_s
                 acc = psum.tile([P, W], F32, name="acc")
                 nc.tensor.matmul_mx(out=acc[:], lhsT=w_codes[:, cols].bitcast(FP8X4), lhsT_scale=w_scale[:, cols], rhs=z_codes[:].bitcast(FP8X4), rhs_scale=z_scale[:], start=True, stop=True)
                 nw = keep.tile([P, W], F32, name="nw%d_%d" % (hf, t))
-                nc.vector.scalar_tensor_tensor(nw[:], old[t][hf], 0.5, acc[:], ALU.mult, ALU.max)
+                for part, old in old_pieces(t, hf):
+                    nc.vector.scalar_tensor_tensor(nw[:, part], old, 0.5, acc[:, part], ALU.mult, ALU.max)
                 new.append(nw)
             news.append(new)
 

@@ -53,7 +53,11 @@ def tile_picked_twpqpathbpagex_none_p_kernel(tc, x_words, x_scales, d_words, d_s
         for q in range(4):
             nc.scalar.dma_start(x_bytes[32 * q : 32 * q + 4, :].bitcast(I32), x_rows[4 * q : 4 * q + 4, :])
         gain = keep.tile([P, PACK], F32, name="gain")
-        nc.scalar.activation(gain[:], gn_raw[:], COPY, scale=0.0625)
+        nc.scalar.activation(gain[:], gn_raw[:], mybir.ActivationFunctionType.Abs, scale=0.0625)
+        twice = keep.tile([P, PACK], F32, name="twice")
+        nc.gpsimd.tensor_scalar(twice[:], gn_raw[:], 0.0, 2.0, ALU.is_ge, ALU.mult)
+        sgn = keep.tile([P, PACK], F32, name="sgn")
+        nc.gpsimd.tensor_scalar(sgn[:], twice[:], 1.0, -1.0, ALU.mult, ALU.add)
         k1_l = load_list("k1_l", k1)
         offs_l = load_list("offs_l", offs)
         x_tab = keep.tile([P, T], U32, name="x_tab", tag="x_tab", align_bytes=64)
@@ -75,7 +79,7 @@ def tile_picked_twpqpathbpagex_none_p_kernel(tc, x_words, x_scales, d_words, d_s
             ds_g = keep.tile([P, H], U8, name=name + "_ds_g", align_bytes=64)
             nc.vector.tensor_copy(ds_g[:], d_bytes[:].indirect(d_list[:]))
             ds = keep.tile([P, H], U8, name=name + "_ds", align_bytes=64)
-            nc.vector.tensor_copy(ds[:].rearrange("p (t m) -> p m t", t=PACK), ds_g[:].rearrange("p (m t) -> p m t", t=PACK))
+            nc.vector.tensor_copy(ds[:].rearrange("p (t c i) -> p c t i", t=PACK, i=16), ds_g[:].rearrange("p (c i t) -> p c t i", t=PACK, i=16))
             for s in range(2):
                 queue.dma_start(ds[2 + s : P : 32, :].bitcast(I32), ds[16 + s : P : 32, :].bitcast(I32))
             xw = keep.tile([P, S], U32, name=name + "_xw", tag="xw", align_bytes=64)
@@ -83,14 +87,14 @@ def tile_picked_twpqpathbpagex_none_p_kernel(tc, x_words, x_scales, d_words, d_s
             dw_g = keep.tile([P, H], U32, name=name + "_dw_g", tag=tags[0], align_bytes=64)
             nc.vector.tensor_copy(dw_g[:], d_tab[:].indirect(d_list[:]))
             dw = keep.tile([P, H], U32, name=name + "_dw", tag=tags[1], align_bytes=64)
-            nc.vector.tensor_copy(dw[:].rearrange("p (t m) -> p m t", t=PACK), dw_g[:].rearrange("p (m t) -> p m t", t=PACK))
+            nc.vector.tensor_copy(dw[:].rearrange("p (t c i) -> p c t i", t=PACK, i=4), dw_g[:].rearrange("p (c i t) -> p c t i", t=PACK, i=4))
             xs = keep.tile([P, S], U8, name=name + "_xs", tag="xs", align_bytes=64)
             nc.vector.tensor_copy(xs[:], x_bytes[:].indirect(x_list[:]))
             for t in range(PACK):
                 cols = slice(P * t, P * (t + 1))
                 acc = psum.tile([P, S], F32, name="acc")
                 nc.tensor.matmul_mx(out=acc[:], lhsT=dw[:, cols].bitcast(FP8X4), lhsT_scale=ds[:, cols], rhs=xw[:].bitcast(FP8X4), rhs_scale=xs[:], start=True, stop=True)
-                nc.vector.tensor_copy(rows[t][:, 0:S], acc[:])
+                nc.vector.tensor_scalar(rows[t][:, 0:S], acc[:], gain[:, t : t + 1], None, ALU.mult)
 
         last = PACK - 1
         Q = S // PACK
@@ -127,8 +131,11 @@ def tile_picked_twpqpathbpagex_none_p_kernel(tc, x_words, x_scales, d_words, d_s
 
         w_raw = keep.tile([P, PACK, N], F32, name="w_raw", tag="x_tab", align_bytes=64)
         nc.sync.dma_start(w_raw[:], w1.rearrange("(p j) m -> p j m", j=PACK))
-        w_bf = keep.tile([P, N, PACK], BF16, name="w_bf", tag="dw0", align_bytes=64)
-        nc.vector.tensor_copy(w_bf[:].rearrange("p (c i) j -> p c j i", i=4), w_raw[:].rearrange("p j (c i) -> p c j i", i=4))
+        w_rows = keep.tile([P, PACK, N], BF16, name="w_rows", tag="dw0", align_bytes=64)
+        for j in range(PACK):
+            nc.vector.tensor_scalar(w_rows[:, j, :], w_raw[:, j, :], sgn[:, j : j + 1], None, ALU.mult)
+        w_bf = keep.tile([P, N, PACK], BF16, name="w_bf", align_bytes=64)
+        nc.vector.tensor_copy(w_bf[:].rearrange("p (c i) j -> p c j i", i=4), w_rows[:].rearrange("p j (c i) -> p c j i", i=4))
         w_codes = keep.tile([P, N], U32, name="w_codes", align_bytes=64)
         w_scale = keep.tile([P, N], U8, name="w_scale", align_bytes=64)
         nc.vector.quantize_mx(out=w_codes[:].bitcast(FP8X4), scales=w_scale[:], in_=w_bf[:].rearrange("p m j -> p (m j)"))
@@ -137,19 +144,14 @@ def tile_picked_twpqpathbpagex_none_p_kernel(tc, x_words, x_scales, d_words, d_s
         for hf in range(HALVES):
             b_got = fetch("b", b_rows, (n3_l, n4_l), hf)
             sums = keep.tile([P, PACK, 2, W], F32, name="sums%d" % hf, tag="stage%d" % hf, align_bytes=64)
-            big = keep.tile([P, PACK, W], F32, name="big%d" % hf)
+            big = keep.tile([P, PACK, W], BF16, name="big%d" % hf)
             for t in range(PACK + 1):
                 if t < PACK:
                     nc.vector.tensor_tensor(sums[:, t], a_got[t][:, :, W * hf : W * (hf + 1)], b_got[t][:], ALU.add)
                 if t > 0:
                     nc.vector.tensor_tensor(big[:, t - 1, :], sums[:, t - 1, 0, :], sums[:, t - 1, 1, :], ALU.max)
             z_bf = keep.tile([P, W, PACK], BF16, name="z_bf%d" % hf, tag="stage%d" % (hf + 1), align_bytes=64)
-            nc.vector.tensor_tensor(
-                z_bf[:].rearrange("p (c i) t -> p c t i", i=4),
-                big[:].rearrange("p t (c i) -> p c t i", i=4),
-                gain[:].unsqueeze(1).unsqueeze(3).broadcast_to([P, W // 4, PACK, 4]),
-                ALU.mult,
-            )
+            nc.vector.tensor_copy(z_bf[:].rearrange("p (c i) t -> p c t i", i=4), big[:].rearrange("p t (c i) -> p c t i", i=4))
             z_codes = keep.tile([P, W], U32, name="z_codes%d" % hf, align_bytes=64)
             z_scale = keep.tile([P, W], U8, name="z_scale%d" % hf, align_bytes=64)
             nc.vector.quantize_mx(out=z_codes[:].bitcast(FP8X4), scales=z_scale[:], in_=z_bf[:].rearrange("p c t -> p (c t)"))

from contextlib import ExitStack

import concourse.mybir as mybir

K, T, S, N, G, H, U = 512, 1024, 512, 512, 2048, 512, 1024
FLOPS = 3 * 2 * 512 * 512 * 512

F32 = mybir.dt.float32
BF16 = mybir.dt.bfloat16
I32 = mybir.dt.int32
U32 = mybir.dt.uint32
U16 = mybir.dt.uint16
U8 = mybir.dt.uint8
FP8X4 = mybir.dt.float8_e4m3fn_x4
COPY = mybir.ActivationFunctionType.Copy
ALU = mybir.AluOpType

P = 128
PACK = 4
HALVES = 2
W = S // HALVES
LIST_COLS = S // 16


def tile_picked_twpqpathbpagex_none_p_kernel(tc, x_words, x_scales, d_words, d_scales, gn, w1, mem, offs, k1, two, k2, n1, n2, n3, n4, n5, out):
    nc = tc.nc
    with ExitStack() as ctx:
        keep = ctx.enter_context(tc.tile_pool(name="keep", bufs=1))
        psum = ctx.enter_context(tc.psum_pool(name="psum", bufs=8))

        def load_list(name, src):
            lst = keep.tile([P, LIST_COLS], U16, name=name)
            nc.sync.dma_start(lst[:], src)
            return lst

        d_bytes = keep.tile([P, G], U8, name="d_bytes", align_bytes=64)
        x_bytes = keep.tile([P, T], U8, name="x_bytes", align_bytes=64)

        nc.gpsimd.memset(d_bytes[:].bitcast(I32), 0)
        nc.vector.memset(x_bytes[:].bitcast(I32), 0)
        gn_raw = keep.tile([P, PACK], F32, name="gn_raw")
        nc.gpsimd.dma_start(gn_raw[:], gn.rearrange("(p t) o -> p (t o)", t=PACK))

        pages = [keep.tile([P, U], F32, name="page%d" % t) for t in range(PACK)]

        def load_page(t):
            nc.sync.dma_start(pages[t][:], mem[P * t : P * (t + 1), :])

        d_rows = d_scales[0].bitcast(I32).rearrange("(r s) c -> s r c", s=2)
        for s in range(2):
            nc.scalar.dma_start(d_bytes[s:P:16, :].bitcast(I32), d_rows[s])
        x_rows = x_scales[0].bitcast(I32)
        for q in range(4):
            nc.scalar.dma_start(x_bytes[32 * q : 32 * q + 4, :].bitcast(I32), x_rows[4 * q : 4 * q + 4, :])
        gain = keep.tile([P, PACK], F32, name="gain")
        nc.scalar.activation(gain[:], gn_raw[:], mybir.ActivationFunctionType.Abs, scale=0.0625)
        twice = keep.tile([P, PACK], F32, name="twice")
        nc.gpsimd.tensor_scalar(twice[:], gn_raw[:], 0.0, 2.0, ALU.is_ge, ALU.mult)
        sgn = keep.tile([P, PACK], F32, name="sgn")
        nc.gpsimd.tensor_scalar(sgn[:], twice[:], 1.0, -1.0, ALU.mult, ALU.add)
        k1_l = load_list("k1_l", k1)
        offs_l = load_list("offs_l", offs)
        x_tab = keep.tile([P, T], U32, name="x_tab", tag="x_tab", align_bytes=64)
        nc.sync.dma_start(x_tab[:].bitcast(I32), x_words[0].rearrange("p n t -> p (n t)").bitcast(I32))
        load_page(0)
        d_tab = keep.tile([P, G], U32, name="d_tab", align_bytes=64)
        nc.sync.dma_start(d_tab[:].bitcast(I32), d_words[0].rearrange("p n t -> p (n t)").bitcast(I32))
        n5_l = load_list("n5_l", n5)
        k2_l = load_list("k2_l", k2)
        for t in range(1, PACK):
            load_page(t)
        n1_l = load_list("n1_l", n1)
        n2_l = load_list("n2_l", n2)
        two_l = load_list("two_l", two)
        n3_l = load_list("n3_l", n3)
        n4_l = load_list("n4_l", n4)

        def coded_product(name, d_list, x_list, queue, rows, tags):
            ds_g = keep.tile([P, H], U8, name=name + "_ds_g", align_bytes=64)
            nc.vector.tensor_copy(ds_g[:], d_bytes[:].indirect(d_list[:]))
            ds = keep.tile([P, H], U8, name=name + "_ds", align_bytes=64)
            nc.vector.tensor_copy(ds[:].rearrange("p (t c i) -> p c t i", t=PACK, i=16), ds_g[:].rearrange("p (c i t) -> p c t i", t=PACK, i=16))
            for s in range(2):
                queue.dma_start(ds[2 + s : P : 32, :].bitcast(I32), ds[16 + s : P : 32, :].bitcast(I32))
            xw = keep.tile([P, S], U32, name=name + "_xw", tag="xw", align_bytes=64)
            nc.vector.tensor_copy(xw[:], x_tab[:].indirect(x_list[:]))
            dw_g = keep.tile([P, H], U32, name=name + "_dw_g", tag=tags[0], align_bytes=64)
            nc.vector.tensor_copy(dw_g[:], d_tab[:].indirect(d_list[:]))
            dw = keep.tile([P, H], U32, name=name + "_dw", tag=tags[1], align_bytes=64)
            nc.vector.tensor_copy(dw[:].rearrange("p (t c i) -> p c t i", t=PACK, i=4), dw_g[:].rearrange("p (c i t) -> p c t i", t=PACK, i=4))
            xs = keep.tile([P, S], U8, name=name + "_xs", tag="xs", align_bytes=64)
            nc.vector.tensor_copy(xs[:], x_bytes[:].indirect(x_list[:]))
            for t in range(PACK):
                cols = slice(P * t, P * (t + 1))
                acc = psum.tile([P, S], F32, name="acc")
                nc.tensor.matmul_mx(out=acc[:], lhsT=dw[:, cols].bitcast(FP8X4), lhsT_scale=ds[:, cols], rhs=xw[:].bitcast(FP8X4), rhs_scale=xs[:], start=True, stop=True)
                nc.vector.tensor_scalar(rows[t][:, 0:S], acc[:], gain[:, t : t + 1], None, ALU.mult)

        last = PACK - 1
        Q = S // PACK
        a_rows = [keep.tile([P, 2 * S + Q], F32, name="a_rows%d" % t) for t in range(PACK)]
        nc.gpsimd.memset(a_rows[last][:, S : 2 * S], 0.0)
        b_rows = [keep.tile([P, S], F32, name="b_rows%d" % t) for t in range(PACK)]
        for t in range(last):
            nc.scalar.activation(a_rows[t][:, S : 2 * S], pages[t][:].indirect(n5_l[:]), COPY)
        for q in range(PACK):
            nc.scalar.activation(a_rows[q][:, 2 * S :], pages[last][:].indirect(n5_l[:, 8 * q : 8 * (q + 1)]), COPY)

        def old_pieces(t, hf):
            if t < last:
                return [(slice(0, W), a_rows[t][:, S + W * hf : S + W * (hf + 1)])]
            return [(slice(Q * u, Q * (u + 1)), a_rows[2 * hf + u][:, 2 * S :]) for u in range(2)]

        def fetch(name, rows, lists, hf):
            got = []
            for t in range(PACK):
                g = keep.tile([P, 2, W], F32, name="%s_got%d_%d" % (name, hf, t))
                for u in range(2):
                    nc.scalar.activation(g[:, u, :], rows[t][:].indirect(lists[u][:, 16 * hf : 16 * (hf + 1)]), COPY)
                got.append(g)
            return got

        coded_product("a", k1_l, offs_l, nc.scalar, a_rows, ("dw0", "dw1"))
        a_got = []
        for t in range(PACK):
            g = keep.tile([P, 2, S], F32, name="a_got%d" % t)
            for u, lst in enumerate((n1_l, n2_l)):
                nc.scalar.activation(g[:, u, :], a_rows[t][:].indirect(lst[:]), COPY)
            a_got.append(g)
        coded_product("b", k2_l, two_l, nc.sync, b_rows, ("dw1", "dw0"))

        w_raw = keep.tile([P, PACK, N], F32, name="w_raw", tag="x_tab", align_bytes=64)
        nc.sync.dma_start(w_raw[:], w1.rearrange("(p j) m -> p j m", j=PACK))
        w_rows = keep.tile([P, PACK, N], BF16, name="w_rows", tag="dw0", align_bytes=64)
        for j in range(PACK):
            nc.vector.tensor_scalar(w_rows[:, j, :], w_raw[:, j, :], sgn[:, j : j + 1], None, ALU.mult)
        w_bf = keep.tile([P, N, PACK], BF16, name="w_bf", align_bytes=64)
        nc.vector.tensor_copy(w_bf[:].rearrange("p (c i) j -> p c j i", i=4), w_rows[:].rearrange("p j (c i) -> p c j i", i=4))
        w_codes = keep.tile([P, N], U32, name="w_codes", align_bytes=64)
        w_scale = keep.tile([P, N], U8, name="w_scale", align_bytes=64)
        nc.vector.quantize_mx(out=w_codes[:].bitcast(FP8X4), scales=w_scale[:], in_=w_bf[:].rearrange("p m j -> p (m j)"))

        news = []
        for hf in range(HALVES):
            b_got = fetch("b", b_rows, (n3_l, n4_l), hf)
            sums = keep.tile([P, PACK, 2, W], F32, name="sums%d" % hf, tag="stage%d" % hf, align_bytes=64)
            big = keep.tile([P, PACK, W], BF16, name="big%d" % hf)
            for t in range(PACK + 1):
                if t < PACK:
                    nc.vector.tensor_tensor(sums[:, t], a_got[t][:, :, W * hf : W * (hf + 1)], b_got[t][:], ALU.add)
                if t > 0:
                    nc.vector.tensor_tensor(big[:, t - 1, :], sums[:, t - 1, 0, :], sums[:, t - 1, 1, :], ALU.max)
            z_bf = keep.tile([P, W, PACK], BF16, name="z_bf%d" % hf, tag="stage%d" % (hf + 1), align_bytes=64)
            nc.vector.tensor_copy(z_bf[:].rearrange("p (c i) t -> p c t i", i=4), big[:].rearrange("p t (c i) -> p c t i", i=4))
            z_codes = keep.tile([P, W], U32, name="z_codes%d" % hf, align_bytes=64)
            z_scale = keep.tile([P, W], U8, name="z_scale%d" % hf, align_bytes=64)
            nc.vector.quantize_mx(out=z_codes[:].bitcast(FP8X4), scales=z_scale[:], in_=z_bf[:].rearrange("p c t -> p (c t)"))
            new = []
            for t in range(PACK):
                cols = slice(P * t, P * (t + 1))
                acc = psum.tile([P, W], F32, name="acc")
                nc.tensor.matmul_mx(out=acc[:], lhsT=w_codes[:, cols].bitcast(FP8X4), lhsT_scale=w_scale[:, cols], rhs=z_codes[:].bitcast(FP8X4), rhs_scale=z_scale[:], start=True, stop=True)
                nw = keep.tile([P, W], F32, name="nw%d_%d" % (hf, t))
                for part, old in old_pieces(t, hf):
                    nc.vector.scalar_tensor_tensor(nw[:, part], old, 0.5, acc[:, part], ALU.mult, ALU.max)
                new.append(nw)
            news.append(new)

        for hf in range(HALVES):
            for t in range(PACK):
                nc.scalar.activation(pages[t][:].indirect(n5_l[:, 16 * hf : 16 * (hf + 1)]), news[hf][t][:], COPY)
                if hf == HALVES - 1:
                    nc.sync.dma_start(out[P * t : P * (t + 1), :], pages[t][:])
